import numpy as np, ml_dtypes
CORES = [50,52,122,124]
N = 4
R, L = 4096, 1024
def entries(a): return a.T.reshape(-1)
def pack(v, P): return np.ascontiguousarray(np.asarray(v, np.int32).reshape(-1, P).T)
def lists(rng, how):
    n = N * L
    h, g = rng.integers(0, N, n), rng.permutation(np.repeat(np.arange(N), L))
    if how == "hotrank":
        a, b = rng.permutation(N)[:2]; M = min(R, n); h[:] = a
        g = np.concatenate([np.full(M, b), rng.permutation(np.repeat(np.delete(np.arange(N), [a, b]), L))[:n - M]]).reshape(N, L)[rng.permutation(N)].reshape(-1)
    if how == "third":
        a, b = 1 + rng.permutation(N - 1)[:2]; h, g = (np.arange(n) // L + a) % N, (np.arange(n) // L + b) % N
    d = np.zeros(n, np.int64)
    for q in range(N): m = np.nonzero(g == q)[0]; d[m] = R * q + np.concatenate([[0, R - 1], 1 + rng.permutation(R - 2)])[:len(m)]
    s = R * h + rng.integers(0, R, n)
    if how == "fork": s = R * h + rng.integers(0, R, N)[h]
    if how == "chain":
        for q in range(N):
            m = np.nonzero(h == q)[0]; w = d[g == q]
            s[m] = w[rng.integers(0, len(w), len(m))]
    if how == "gaps":
        z = rng.permutation(N)[:3]; k = (rng.random(n) < 0.5) | (np.arange(n) // L == z[0]) | (h == z[1]) | (g == z[2]); s[k] = -1; d[k] = -1
    return {"src": np.stack([pack(v, 16) for v in s.reshape(N, L)]), "dst": np.stack([pack(v, 16) for v in d.reshape(N, L)])}
def setup_inputs(rng):
    return dict({"tab": rng.standard_normal((N, 128, R), dtype=np.float32).astype(ml_dtypes.bfloat16)}, **lists(rng, "uniform"))
def setup_inputs_chain(rng):
    d = setup_inputs(rng); d.update(lists(rng, "chain"))
    for k in ("tab",): d[k] = (d[k].astype(np.float32) * 1048576.0).astype(d[k].dtype)
    return d
def setup_inputs_fork(rng):
    d = setup_inputs(rng); d.update(lists(rng, "fork"))
    for k in ("tab",): d[k] = (d[k].astype(np.float32) * (1 / 1024.0)).astype(d[k].dtype)
    return d
def setup_inputs_gaps(rng):
    d = setup_inputs(rng); d.update(lists(rng, "gaps"))
    return d
def setup_inputs_hotrank(rng):
    d = setup_inputs(rng); d.update(lists(rng, "hotrank"))
    return d
def setup_inputs_third(rng):
    d = setup_inputs(rng); d.update(lists(rng, "third"))
    return d
def check_inputs(x):
    bad = []; s, d = x["src"].reshape(-1), x["dst"].reshape(-1); k = d >= 0
    if s.min() < -1 or s.max() >= N * R or d.min() < -1 or d.max() >= N * R: bad.append("out of range")
    if ((s < 0) != (d < 0)).any(): bad.append("half a pair")
    if len(np.unique(d[k])) != int(k.sum()): bad.append("a column is written twice")
    return bad
def reference(tab, src, dst):
    A = np.concatenate(list(tab), axis=1); Y = A.copy()
    for r in range(N):
        s, d = entries(src[r]), entries(dst[r]); k = d >= 0
        Y[:, d[k]] = A[:, s[k]]
    return {"y": np.stack([Y[:, R * r:R * r + R] for r in range(N)])}

@@ -1,0 +1,224 @@
+from concourse.bass import DstId, RemoteDMATransfer
+from concourse.mybir import dt, AluOpType, ActivationFunctionType
+
+R = 4096
+NR = 4
+H = R // 2
+PIECES = 2
+W = H // PIECES
+GCH = 1024
+
+SCRATCH = {
+    "win": ("sbuf", [128, NR * R], "bfloat16"),
+    "yb": ("sbuf", [128, R], "bfloat16"),
+    "lt": ("sbuf", [128, NR * 16], "int32"),
+    "ei": ("sbuf", [128, 2 * NR * 16], "int32"),
+    "eb": ("sbuf", [128, 2 * NR * 16], "bfloat16"),
+    "ab": ("sbuf", [128, 2 * NR * 8], "bfloat16"),
+    "oh": ("sbuf", [128, 32 * 128], "bfloat16"),
+    "rh": ("sbuf", [128, 32 * 64], "bfloat16"),
+    "i128": ("sbuf", [128, 128], "bfloat16"),
+    "iq": ("sbuf", [128, 128], "bfloat16"),
+    "kc": ("sbuf", [128, 8], "bfloat16"),
+    "own": ("sbuf", [128, 64], "bfloat16"),
+    "sel": ("sbuf", [128, 8 * 128], "bfloat16"),
+    "inv": ("sbuf", [128, 64], "bfloat16"),
+    "off": ("sbuf", [128, 256], "uint16"),
+    "nz": ("sbuf", [128, 1], "float32"),
+    "psa": ("psum", [128, 512], "float32"),
+    "psb": ("psum", [128, 512], "float32"),
+}
+SEMAPHORES = (["lst", "lnear", "lfar", "fin", "sent", "sg", "sv", "ss", "sp", "st"]
+              + ["%s%d" % (k, i) for k in ("ld", "x", "y") for i in range(PIECES)])
+
+
+def bits(mask):
+    return [1 << b for b in range(mask.bit_length()) if mask >> b & 1]
+
+
+def part(mask, i, n):
+    b = bits(mask)
+    k = len(b) // n
+    return sum(b[i * k:(i + 1) * k])
+
+
+def roles(cores, topo):
+    allc = range(topo.CHIPS * topo.CORES_PER_CHIP)
+    out = {}
+    for s in cores:
+        mate = [c for c in cores if c != s and topo.chip(c) == topo.chip(s)][0]
+        far = [c for c in cores if topo.chip(c) != topo.chip(s)]
+        p = [c for c in far if topo.die(c) == topo.die(s)][0]
+        q = [c for c in far if c != p][0]
+        relay = [c for c in allc if topo.mates(topo.chip(c), topo.chip(p)) and topo.same_plane(topo.chip(c), topo.chip(s))
+                 and topo.die(c) == topo.die(s) and topo.may_write(c, p) and topo.may_write(s, c)][0]
+        direct = s if topo.may_write(s, p) else [
+            c for c in allc if topo.chip(c) == topo.chip(s) and topo.die(c) == topo.die(s)
+            and c not in cores and topo.may_write(c, p)][0]
+        out[s] = {"mate": mate, "p": p, "q": q, "relay": relay, "direct": direct}
+    return out
+
+
+def plan(cores, topo):
+    ro = roles(cores, topo)
+    calls, total = {}, {}
+
+    def call(core, after, transfers):
+        calls.setdefault(core, []).append((after, transfers))
+        for d, m, sem, buf, a, b in transfers:
+            total[d, sem] = total.get((d, sem), 0) + len(bits(m))
+
+    for r, s in enumerate(cores):
+        o = ro[s]
+        mate, p, q, relay, direct = o["mate"], o["p"], o["q"], o["relay"], o["direct"]
+        offm = topo.mask(s, relay)
+        onm = topo.mask(s, mate) & ~offm
+        la, lb = 16 * r, 16 * r + 16
+        total[s, "lst"] = 32
+        for i in range(PIECES):
+            total[s, "ld%d" % i] = 32
+        X = [(R * r + W * i, R * r + W * i + W) for i in range(PIECES)]
+        Y = [(R * r + H + W * i, R * r + H + W * i + W) for i in range(PIECES)]
+        if direct == s:
+            call(s, ["lst"], [(p, part(offm, 0, 2), "lfar", "lt", la, lb),
+                              (relay, part(offm, 1, 2), "lfar", "lt", la, lb),
+                              (mate, onm, "lnear", "lt", la, lb)])
+            for i in range(PIECES):
+                call(s, ["ld%d" % i], [(p, part(offm, 0, 2), "x%d" % i, "win") + X[i],
+                                       (relay, part(offm, 1, 2), "y%d" % i, "win") + Y[i],
+                                       (mate, part(onm, 0, 2), "fin", "win") + X[i],
+                                       (mate, part(onm, 1, 2), "fin", "win") + Y[i]])
+        else:
+            call(s, ["lst"], [(relay, offm, "lfar", "lt", la, lb),
+                              (direct, part(onm, 0, 2), "lfar", "lt", la, lb),
+                              (mate, part(onm, 1, 2), "lnear", "lt", la, lb)])
+            for i in range(PIECES):
+                call(s, ["ld%d" % i], [(relay, offm, "y%d" % i, "win") + Y[i],
+                                       (direct, part(onm, 0, 2), "x%d" % i, "win") + X[i],
+                                       (mate, part(onm, 1, 2), "fin", "win") + Y[i]])
+            dm = topo.mask(direct, p)
+            call(direct, ["lfar"], [(p, dm, "lfar", "lt", la, lb)])
+            for i in range(PIECES):
+                call(direct, ["x%d" % i], [(p, dm, "x%d" % i, "win") + X[i]])
+            call(direct, [], [(mate, topo.mask(direct, mate) & ~dm, "fin", "win", X[0][0], X[-1][1])])
+        rm = topo.mask(relay, p)
+        call(relay, ["lfar"], [(q, rm, "lfar", "lt", la, lb)])
+        for i in range(PIECES):
+            call(relay, ["y%d" % i], [(p, rm, "y%d" % i, "win") + Y[i]])
+    for r, s in enumerate(cores):
+        p, q = ro[s]["p"], ro[s]["q"]
+        for k, off in (("x", 0), ("y", H)):
+            for i in range(PIECES):
+                a = R * r + off + W * i
+                call(p, ["%s%d" % (k, i)], [(q, topo.mask(p, q), "fin", "win", a, a + W)])
+    return calls, total
+
+
+def rank_program(g, core, T, topo):
+    cores = list(T.cores)
+    calls, total = plan(cores, topo)
+    rank = T.rank_of(core)
+    if rank is None and core not in calls:
+        return
+    if rank is not None:
+        near = [r for r in range(NR) if topo.chip(cores[r]) == topo.chip(core)]
+        far = [r for r in range(NR) if r not in near]
+        compute(g, core, rank, near, far, T, total)
+    sent = 0
+    for after, transfers in calls[core]:
+        for sem in after:
+            g.wait_ge(T.sem[sem], total[core, sem])
+        ts = []
+        for d, m, sem, buf, a, b in transfers:
+            rid, pid, _ = topo.addr(d)
+            ts.append(RemoteDMATransfer(dst_ids=[DstId(rid=rid, pnc=pid)], dma_engine_mask=m, remote_sem=T.sem[sem],
+                                        src=T[buf][:, a:b], dst=T[buf][:, a:b]))
+            sent += len(bits(m))
+        g.remote_dma_fused(ts, local_sem=T.sem.sent)
+    g.wait_ge(T.sem.sent, sent)
+
+
+def compute(g, core, rank, near, far, T, total):
+    A = AluOpType
+    v, base = g.vector, R * rank
+    g.sync.dma_start(T.lt[:, 16 * rank:16 * rank + 8], T.src[:]).then_inc(T.sem.lst, 16)
+    g.scalar.dma_start(T.lt[:, 16 * rank + 8:16 * rank + 16], T.dst[:]).then_inc(T.sem.lst, 16)
+    for i in range(PIECES):
+        for queue, o in ((g.sync, W * i), (g.scalar, H + W * i)):
+            queue.dma_start(T.win[:, base + o:base + o + W], T.tab[:, o:o + W]).then_inc(T.sem["ld%d" % i], 16)
+    g.iota(T.iq[:], [[0, 8], [1, 16]], 0, 0, allow_small_or_imprecise_dtypes=True).then_inc(T.sem.sg, 1)
+    g.iota(T.kc[:], [[-16, 8]], 0, 1, allow_small_or_imprecise_dtypes=True).then_inc(T.sem.sg, 1)
+    g.iota(T.i128[:], [[1, 128]], 0, 0, allow_small_or_imprecise_dtypes=True).then_inc(T.sem.sg, 1)
+    g.iota(T.own[:, 0:32], [[128, 32]], base, 0, allow_small_or_imprecise_dtypes=True).then_inc(T.sem.sg, 1)
+    g.iota(T.own[:, 32:64], [[0, 32]], 0, 1, allow_small_or_imprecise_dtypes=True).then_inc(T.sem.sg, 1)
+
+    vn = [0]
+
+    def vi(ins):
+        vn[0] += 1
+        ins.then_inc(T.sem.sv, 1)
+        return vn[0]
+
+    def vwait():
+        v.wait_ge(T.sem.sv, vn[0])
+
+    vi(v.memset(T.nz[:], -0.0))
+    v.wait_ge(T.sem.sg, 5)
+    for u in range(8):
+        vi(v.tensor_scalar(T.sel[:, 128 * u:128 * u + 128], T.iq[:], T.kc[:, u:u + 1], None, A.is_equal))
+    done = []
+    NB = NR * 16
+    for batch, sems in ((near, ["lst", "lnear"]), (far, ["lfar"])):
+        for s in sems:
+            v.wait_ge(T.sem[s], total[core, s])
+        a, b = 16 * batch[0], 16 * batch[-1] + 16
+        vi(v.tensor_scalar(T.ei[:, a:b], T.lt[:, a:b], 127, None, A.bitwise_and))
+        vi(v.tensor_scalar(T.ei[:, NB + a:NB + b], T.lt[:, a:b], (NR * R - 1) & ~127, None, A.bitwise_and))
+        vwait()
+        vi(v.tensor_copy(T.eb[:, a:b], T.ei[:, a:b]))
+        vi(v.tensor_copy(T.eb[:, NB + a:NB + b], T.ei[:, NB + a:NB + b]))
+        for r in batch:
+            for o, e in ((0, NB + 16 * r), (NR * 8, 16 * r)):
+                vi(v.tensor_tensor(T.ab[:, o + 8 * r:o + 8 * r + 8], T.ei[:, e:e + 8], T.ei[:, e + 8:e + 16], A.subtract))
+        vwait()
+        for r in batch:
+            for t in range(8):
+                j, lo = 8 * r + t, 16 * r + 8 + t
+                vi(v.tensor_scalar(T.oh[:, 128 * j:128 * j + 128], T.i128[:], T.eb[:, lo:lo + 1], None, A.is_equal))
+                for o in (0, NR * 8):
+                    c = 64 * j + o
+                    vi(v.tensor_scalar(T.rh[:, c:c + 32], T.own[:, 0:32], T.eb[:, NB + lo:NB + lo + 1],
+                                       T.ab[:, o + j:o + j + 1], A.is_equal, A.mult))
+                done.append((j, vn[0]))
+    for k, (j, n) in enumerate(done):
+        if k % 2 == 0:
+            g.tensor.wait_ge(T.sem.sv, done[k + 1][1])
+        g.tensor.matmul(T.psa[:, 0:64], T.oh[:, 128 * j:128 * j + 128], T.rh[:, 64 * j:64 * j + 64],
+                        k == 0, k == len(done) - 1).then_inc(T.sem.sp, 1)
+    v.wait_ge(T.sem.sp, len(done))
+    n = vi(v.tensor_tensor(T.inv[:], T.psa[:, 0:64], T.own[:], A.add))
+    g.tensor.wait_ge(T.sem.sv, n)
+    for u in range(8):
+        s = T.sel[:, 128 * u:128 * u + 128]
+        g.tensor.matmul(T.psb[:, u:256:8], s, T.inv[:, 0:32], True, False).then_inc(T.sem.sp, 1)
+        g.tensor.matmul(T.psb[:, u:256:8], s, T.inv[:, 32:64], False, True).then_inc(T.sem.sp, 1)
+    v.wait_ge(T.sem.sp, len(done) + 16)
+    noff = vi(v.tensor_copy(T.off[:], T.psb[:, 0:256]))
+
+    data = ["ld%d" % i for i in range(PIECES)] + ["%s%d" % (k, i) for k in ("x", "y") for i in range(PIECES)] + ["fin"]
+    for queue in (v, g.scalar):
+        queue.wait_ge(T.sem.sv, noff)
+        for s in data:
+            queue.wait_ge(T.sem[s], total[core, s])
+    stores = 0
+    for i in range(H // GCH):
+        a = GCH * i
+        n = vi(v.tensor_copy(T.yb[:, a:a + GCH], T.win[:, 0:NR * R].indirect(T.off[:, a // 16:(a + GCH) // 16])))
+        b = H + a
+        g.scalar.activation(T.yb[:, b:b + GCH], T.win[:, 0:NR * R].indirect(T.off[:, b // 16:(b + GCH) // 16]),
+                            ActivationFunctionType.Identity, bias=T.nz[:, 0:1], scale=1.0).then_inc(T.sem.ss, 1)
+        for sem, k, c in ((T.sem.sv, n, a), (T.sem.ss, i + 1, b)):
+            g.sync.wait_ge(sem, k)
+            g.sync.dma_start(T.y[:, c:c + GCH], T.yb[:, c:c + GCH]).then_inc(T.sem.st, 16)
+            stores += 16
+    g.sync.wait_ge(T.sem.st, stores)

@@ -4,32 +4,41 @@ from concourse.mybir import dt, AluOpType, ActivationFunctionType
 R = 4096
 NR = 4
 H = R // 2
-PIECES = 2
-W = H // PIECES
-GCH = 1024
+SIZES = (256, 704, 640, 448)
+NP = len(SIZES)
+AT = [sum(SIZES[:i]) for i in range(NP + 1)]
+JOIN = (0, 2, NP - 1)
+CHUNKS = (832, 704, 512)
+DW = 64
 
 SCRATCH = {
     "win": ("sbuf", [128, NR * R], "bfloat16"),
     "yb": ("sbuf", [128, R], "bfloat16"),
-    "lt": ("sbuf", [128, NR * 16], "int32"),
-    "ei": ("sbuf", [128, 2 * NR * 16], "int32"),
-    "eb": ("sbuf", [128, 2 * NR * 16], "bfloat16"),
-    "ab": ("sbuf", [128, 2 * NR * 8], "bfloat16"),
-    "oh": ("sbuf", [128, 32 * 128], "bfloat16"),
-    "rh": ("sbuf", [128, 32 * 64], "bfloat16"),
+    "lt": ("sbuf", [128, 16], "int32"),
+    "ei": ("sbuf", [128, 32], "int32"),
+    "eb": ("sbuf", [128, 16], "bfloat16"),
+    "ab": ("sbuf", [128, 16], "bfloat16"),
+    "oh": ("sbuf", [128, 8 * 128], "bfloat16"),
+    "rh": ("sbuf", [128, 8 * 256], "bfloat16"),
     "i128": ("sbuf", [128, 128], "bfloat16"),
+    "h128": ("sbuf", [128, 128], "bfloat16"),
     "iq": ("sbuf", [128, 128], "bfloat16"),
     "kc": ("sbuf", [128, 8], "bfloat16"),
-    "own": ("sbuf", [128, 64], "bfloat16"),
+    "own": ("sbuf", [128, DW], "bfloat16"),
     "sel": ("sbuf", [128, 8 * 128], "bfloat16"),
-    "inv": ("sbuf", [128, 64], "bfloat16"),
+    "dd": ("sbuf", [128, NR * DW], "bfloat16"),
+    "dr": ("sbuf", [128, NR * DW], "bfloat16"),
+    "inv0": ("sbuf", [128, DW], "bfloat16"),
+    "inv1": ("sbuf", [128, DW], "bfloat16"),
+    "dfar": ("sbuf", [128, DW], "bfloat16"),
+    "inv": ("sbuf", [128, DW], "bfloat16"),
     "off": ("sbuf", [128, 256], "uint16"),
     "nz": ("sbuf", [128, 1], "float32"),
     "psa": ("psum", [128, 512], "float32"),
     "psb": ("psum", [128, 512], "float32"),
 }
-SEMAPHORES = (["lst", "lnear", "lfar", "fin", "sent", "sg", "sv", "ss", "sp", "st"]
-              + ["%s%d" % (k, i) for k in ("ld", "x", "y") for i in range(PIECES)])
+SEMAPHORES = (["lst", "dd", "dn", "df", "fin", "sent", "sg", "sv", "ss", "sp", "st"]
+              + ["%s%d" % (k, i) for k in ("ld", "x", "y", "fw") for i in range(NP)])
 
 
 def bits(mask):
@@ -52,10 +61,9 @@ def roles(cores, topo):
         q = [c for c in far if c != p][0]
         relay = [c for c in allc if topo.mates(topo.chip(c), topo.chip(p)) and topo.same_plane(topo.chip(c), topo.chip(s))
                  and topo.die(c) == topo.die(s) and topo.may_write(c, p) and topo.may_write(s, c)][0]
-        direct = s if topo.may_write(s, p) else [
-            c for c in allc if topo.chip(c) == topo.chip(s) and topo.die(c) == topo.die(s)
-            and c not in cores and topo.may_write(c, p)][0]
-        out[s] = {"mate": mate, "p": p, "q": q, "relay": relay, "direct": direct}
+        port = [c for c in allc if topo.chip(c) == topo.chip(s) and topo.die(c) == topo.die(s)
+                and c not in cores and topo.may_write(c, p)][0]
+        out[s] = {"mate": mate, "p": p, "q": q, "relay": relay, "port": port}
     return out
 
 
@@ -65,52 +73,56 @@ def plan(cores, topo):
 
     def call(core, after, transfers):
         calls.setdefault(core, []).append((after, transfers))
-        for d, m, sem, buf, a, b in transfers:
-            total[d, sem] = total.get((d, sem), 0) + len(bits(m))
+        for t in transfers:
+            total[t[0], t[2]] = total.get((t[0], t[2]), 0) + len(bits(t[1]))
+
+    def win(dst, mask, sem, a, b):
+        return (dst, mask, sem, "win", a, b, "win", a)
 
     for r, s in enumerate(cores):
         o = ro[s]
-        mate, p, q, relay, direct = o["mate"], o["p"], o["q"], o["relay"], o["direct"]
+        mate, p, q, relay, port = o["mate"], o["p"], o["q"], o["relay"], o["port"]
         offm = topo.mask(s, relay)
-        onm = topo.mask(s, mate) & ~offm
-        la, lb = 16 * r, 16 * r + 16
+        allm = topo.mask(s, mate)
+        onm = allm & ~offm
         total[s, "lst"] = 32
-        for i in range(PIECES):
+        for i in range(NP):
             total[s, "ld%d" % i] = 32
-        X = [(R * r + W * i, R * r + W * i + W) for i in range(PIECES)]
-        Y = [(R * r + H + W * i, R * r + H + W * i + W) for i in range(PIECES)]
-        if direct == s:
-            call(s, ["lst"], [(p, part(offm, 0, 2), "lfar", "lt", la, lb),
-                              (relay, part(offm, 1, 2), "lfar", "lt", la, lb),
-                              (mate, onm, "lnear", "lt", la, lb)])
-            for i in range(PIECES):
-                call(s, ["ld%d" % i], [(p, part(offm, 0, 2), "x%d" % i, "win") + X[i],
-                                       (relay, part(offm, 1, 2), "y%d" % i, "win") + Y[i],
-                                       (mate, part(onm, 0, 2), "fin", "win") + X[i],
-                                       (mate, part(onm, 1, 2), "fin", "win") + Y[i]])
-        else:
-            call(s, ["lst"], [(relay, offm, "lfar", "lt", la, lb),
-                              (direct, part(onm, 0, 2), "lfar", "lt", la, lb),
-                              (mate, part(onm, 1, 2), "lnear", "lt", la, lb)])
-            for i in range(PIECES):
-                call(s, ["ld%d" % i], [(relay, offm, "y%d" % i, "win") + Y[i],
-                                       (direct, part(onm, 0, 2), "x%d" % i, "win") + X[i],
-                                       (mate, part(onm, 1, 2), "fin", "win") + Y[i]])
-            dm = topo.mask(direct, p)
-            call(direct, ["lfar"], [(p, dm, "lfar", "lt", la, lb)])
-            for i in range(PIECES):
-                call(direct, ["x%d" % i], [(p, dm, "x%d" % i, "win") + X[i]])
-            call(direct, [], [(mate, topo.mask(direct, mate) & ~dm, "fin", "win", X[0][0], X[-1][1])])
-        rm = topo.mask(relay, p)
-        call(relay, ["lfar"], [(q, rm, "lfar", "lt", la, lb)])
-        for i in range(PIECES):
-            call(relay, ["y%d" % i], [(p, rm, "y%d" % i, "win") + Y[i]])
+        X = [(R * r + AT[i], R * r + AT[i + 1]) for i in range(NP)]
+        Y = [(H + a, H + b) for a, b in X]
+
+        def D(dst, mask, sem, d, buf, c):
+            return (dst, mask, sem, "dd", DW * d, DW * d + DW, buf, c)
+
+        rp, rq, rm = cores.index(p), cores.index(q), cores.index(mate)
+        last = NP - 1
+        for i in range(NP):
+            if i == last:
+                call(s, ["D"], [D(relay, part(offm, 0, 2), "dd", rp, "dd", DW * rp),
+                                D(relay, part(offm, 1, 2), "dd", rq, "dd", DW * rq),
+                                D(mate, onm, "dn", rm, "dr", DW * r)])
+            call(s, ["ld%d" % i], [win(relay, offm, "y%d" % i, *Y[i]), win(port, onm, "x%d" % i, *X[i])])
+        call(s, [], [win(mate, allm, "fin", Y[0][0], Y[-1][1])])
+        pm, rm = topo.mask(port, p), topo.mask(relay, p)
+        po = topo.mask(port, mate) & ~pm
+        for k in range(len(JOIN) - 1):
+            for i in range(JOIN[k], JOIN[k + 1]):
+                if i == 0:
+                    call(port, ["x0"], [win(p, pm, "fw0", *X[0])])
+                    call(port, [], [win(mate, po, "fin", *X[0])])
+                else:
+                    call(port, ["x%d" % i], [win(p, pm, "fw%d" % k, *X[i]), win(mate, po, "fin", *X[i])])
+                call(relay, ["y%d" % i], [win(p, rm, "fw%d" % k, *Y[i])])
+        call(port, ["x%d" % last], [win(p, part(pm, 0, 2), "fin", *X[last]), win(q, part(pm, 1, 2), "fin", *X[last]),
+                                    win(mate, po, "fin", *X[last])])
+        call(relay, ["dd"], [D(p, part(rm, 0, 2), "df", rp, "dr", DW * r), D(q, part(rm, 1, 2), "df", rq, "dr", DW * r)])
+        call(relay, ["y%d" % last], [win(p, part(rm, 0, 2), "fin", *Y[last]), win(q, part(rm, 1, 2), "fin", *Y[last])])
     for r, s in enumerate(cores):
         p, q = ro[s]["p"], ro[s]["q"]
-        for k, off in (("x", 0), ("y", H)):
-            for i in range(PIECES):
-                a = R * r + off + W * i
-                call(p, ["%s%d" % (k, i)], [(q, topo.mask(p, q), "fin", "win", a, a + W)])
+        m = topo.mask(p, q)
+        for k in range(len(JOIN) - 1):
+            a, b = R * r + AT[JOIN[k]], R * r + AT[JOIN[k + 1]]
+            call(p, ["fw%d" % k], [win(q, part(m, 0, 2), "fin", a, b), win(q, part(m, 1, 2), "fin", H + a, H + b)])
     return calls, total
 
 
@@ -120,19 +132,23 @@ def rank_program(g, core, T, topo):
     rank = T.rank_of(core)
     if rank is None and core not in calls:
         return
+    made = 0
     if rank is not None:
-        near = [r for r in range(NR) if topo.chip(cores[r]) == topo.chip(core)]
-        far = [r for r in range(NR) if r not in near]
-        compute(g, core, rank, near, far, T, total)
+        near = [r for r in range(NR) if topo.chip(cores[r]) == topo.chip(core) and r != rank]
+        far = [r for r in range(NR) if topo.chip(cores[r]) != topo.chip(core)]
+        made = compute(g, core, rank, near[0], far, T, total)
     sent = 0
     for after, transfers in calls[core]:
         for sem in after:
-            g.wait_ge(T.sem[sem], total[core, sem])
+            if sem == "D":
+                g.wait_ge(T.sem.sv, made)
+            else:
+                g.wait_ge(T.sem[sem], total[core, sem])
         ts = []
-        for d, m, sem, buf, a, b in transfers:
+        for d, m, sem, buf, a, b, dbuf, da in transfers:
             rid, pid, _ = topo.addr(d)
             ts.append(RemoteDMATransfer(dst_ids=[DstId(rid=rid, pnc=pid)], dma_engine_mask=m, remote_sem=T.sem[sem],
-                                        src=T[buf][:, a:b], dst=T[buf][:, a:b]))
+                                        src=T[buf][:, a:b], dst=T[dbuf][:, da:da + b - a]))
             sent += len(bits(m))
         g.remote_dma_fused(ts, local_sem=T.sem.sent)
     g.wait_ge(T.sem.sent, sent)
@@ -141,16 +157,15 @@ def rank_program(g, core, T, topo):
 def compute(g, core, rank, near, far, T, total):
     A = AluOpType
     v, base = g.vector, R * rank
-    g.sync.dma_start(T.lt[:, 16 * rank:16 * rank + 8], T.src[:]).then_inc(T.sem.lst, 16)
-    g.scalar.dma_start(T.lt[:, 16 * rank + 8:16 * rank + 16], T.dst[:]).then_inc(T.sem.lst, 16)
-    for i in range(PIECES):
-        for queue, o in ((g.sync, W * i), (g.scalar, H + W * i)):
-            queue.dma_start(T.win[:, base + o:base + o + W], T.tab[:, o:o + W]).then_inc(T.sem["ld%d" % i], 16)
-    g.iota(T.iq[:], [[0, 8], [1, 16]], 0, 0, allow_small_or_imprecise_dtypes=True).then_inc(T.sem.sg, 1)
-    g.iota(T.kc[:], [[-16, 8]], 0, 1, allow_small_or_imprecise_dtypes=True).then_inc(T.sem.sg, 1)
+    g.sync.dma_start(T.lt[:, 0:8], T.src[:]).then_inc(T.sem.lst, 16)
+    g.scalar.dma_start(T.lt[:, 8:16], T.dst[:]).then_inc(T.sem.lst, 16)
+    for i in range(NP):
+        for queue, o in ((g.sync, 0), (g.scalar, H)):
+            a, b = o + AT[i], o + AT[i + 1]
+            queue.dma_start(T.win[:, base + a:base + b], T.tab[:, a:b]).then_inc(T.sem["ld%d" % i], 16)
     g.iota(T.i128[:], [[1, 128]], 0, 0, allow_small_or_imprecise_dtypes=True).then_inc(T.sem.sg, 1)
-    g.iota(T.own[:, 0:32], [[128, 32]], base, 0, allow_small_or_imprecise_dtypes=True).then_inc(T.sem.sg, 1)
-    g.iota(T.own[:, 32:64], [[0, 32]], 0, 1, allow_small_or_imprecise_dtypes=True).then_inc(T.sem.sg, 1)
+    g.iota(T.kc[:], [[-16, 8]], 0, 1, allow_small_or_imprecise_dtypes=True).then_inc(T.sem.sg, 1)
+    g.iota(T.iq[:], [[0, 8], [1, 16]], 0, 0, allow_small_or_imprecise_dtypes=True).then_inc(T.sem.sg, 1)
 
     vn = [0]
 
@@ -163,62 +178,67 @@ def compute(g, core, rank, near, far, T, total):
         v.wait_ge(T.sem.sv, vn[0])
 
     vi(v.memset(T.nz[:], -0.0))
-    v.wait_ge(T.sem.sg, 5)
+    v.wait_ge(T.sem.sg, 3)
+    vi(v.tensor_scalar(T.h128[:], T.i128[:], 128.0, None, A.mult))
     for u in range(8):
         vi(v.tensor_scalar(T.sel[:, 128 * u:128 * u + 128], T.iq[:], T.kc[:, u:u + 1], None, A.is_equal))
-    done = []
-    NB = NR * 16
-    for batch, sems in ((near, ["lst", "lnear"]), (far, ["lfar"])):
-        for s in sems:
-            v.wait_ge(T.sem[s], total[core, s])
-        a, b = 16 * batch[0], 16 * batch[-1] + 16
-        vi(v.tensor_scalar(T.ei[:, a:b], T.lt[:, a:b], 127, None, A.bitwise_and))
-        vi(v.tensor_scalar(T.ei[:, NB + a:NB + b], T.lt[:, a:b], (NR * R - 1) & ~127, None, A.bitwise_and))
-        vwait()
-        vi(v.tensor_copy(T.eb[:, a:b], T.ei[:, a:b]))
-        vi(v.tensor_copy(T.eb[:, NB + a:NB + b], T.ei[:, NB + a:NB + b]))
-        for r in batch:
-            for o, e in ((0, NB + 16 * r), (NR * 8, 16 * r)):
-                vi(v.tensor_tensor(T.ab[:, o + 8 * r:o + 8 * r + 8], T.ei[:, e:e + 8], T.ei[:, e + 8:e + 16], A.subtract))
-        vwait()
-        for r in batch:
-            for t in range(8):
-                j, lo = 8 * r + t, 16 * r + 8 + t
-                vi(v.tensor_scalar(T.oh[:, 128 * j:128 * j + 128], T.i128[:], T.eb[:, lo:lo + 1], None, A.is_equal))
-                for o in (0, NR * 8):
-                    c = 64 * j + o
-                    vi(v.tensor_scalar(T.rh[:, c:c + 32], T.own[:, 0:32], T.eb[:, NB + lo:NB + lo + 1],
-                                       T.ab[:, o + j:o + j + 1], A.is_equal, A.mult))
-                done.append((j, vn[0]))
-    for k, (j, n) in enumerate(done):
-        if k % 2 == 0:
-            g.tensor.wait_ge(T.sem.sv, done[k + 1][1])
-        g.tensor.matmul(T.psa[:, 0:64], T.oh[:, 128 * j:128 * j + 128], T.rh[:, 64 * j:64 * j + 64],
-                        k == 0, k == len(done) - 1).then_inc(T.sem.sp, 1)
-    v.wait_ge(T.sem.sp, len(done))
-    n = vi(v.tensor_tensor(T.inv[:], T.psa[:, 0:64], T.own[:], A.add))
+    vwait()
+    vi(v.tensor_copy(T.own[:, 0:DW:2], T.h128[:, 32 * rank:32 * rank + 32]))
+    vi(v.tensor_scalar(T.own[:, 1:DW:2], T.h128[:, 0:32], 0.0, T.kc[:, 0:1], A.mult, A.add))
+    v.wait_ge(T.sem.lst, total[core, "lst"])
+    vi(v.tensor_scalar(T.ei[:, 0:32:2], T.lt[:], 127, None, A.bitwise_and))
+    vi(v.tensor_scalar(T.ei[:, 1:32:2], T.lt[:], (NR * R - 1) & ~127, None, A.bitwise_and))
+    vwait()
+    vi(v.tensor_copy(T.eb[:], T.ei[:, 16:32]))
+    vi(v.tensor_tensor(T.ab[:], T.ei[:, 0:16], T.ei[:, 16:32], A.subtract))
+    vwait()
+    for t in range(8):
+        lo, hi, c = 2 * t, 2 * t + 1, 256 * t
+        vi(v.tensor_scalar(T.oh[:, 128 * t:128 * t + 128], T.i128[:], T.eb[:, lo:lo + 1], None, A.is_equal))
+        vi(v.tensor_scalar(T.rh[:, c:c + 256:2], T.h128[:], T.eb[:, hi:hi + 1], T.ab[:, hi:hi + 1], A.is_equal, A.mult))
+        n = vi(v.tensor_scalar(T.rh[:, c + 1:c + 256:2], T.h128[:], T.eb[:, hi:hi + 1], T.ab[:, lo:lo + 1],
+                               A.is_equal, A.mult))
+        g.tensor.wait_ge(T.sem.sv, n)
+        g.tensor.matmul(T.psa[:, 0:256], T.oh[:, 128 * t:128 * t + 128], T.rh[:, c:c + 256],
+                        t == 0, t == 7).then_inc(T.sem.sp, 1)
+    v.wait_ge(T.sem.sp, 8)
+    made = vi(v.tensor_copy(T.dd[:], T.psa[:, 0:256]))
+    vwait()
+
+    def mine(r):
+        return T.dr[:, DW * r:DW * r + DW]
+
+    vi(v.tensor_tensor(T.inv0[:], T.dd[:, DW * rank:DW * rank + DW], T.own[:], A.add))
+    vwait()
+    v.wait_ge(T.sem.dn, total[core, "dn"])
+    vi(v.tensor_tensor(T.inv1[:], T.inv0[:], mine(near), A.add))
+    v.wait_ge(T.sem.df, total[core, "df"])
+    vi(v.tensor_tensor(T.dfar[:], mine(far[0]), mine(far[1]), A.add))
+    vwait()
+    n = vi(v.tensor_tensor(T.inv[:], T.inv1[:], T.dfar[:], A.add))
     g.tensor.wait_ge(T.sem.sv, n)
     for u in range(8):
         s = T.sel[:, 128 * u:128 * u + 128]
-        g.tensor.matmul(T.psb[:, u:256:8], s, T.inv[:, 0:32], True, False).then_inc(T.sem.sp, 1)
-        g.tensor.matmul(T.psb[:, u:256:8], s, T.inv[:, 32:64], False, True).then_inc(T.sem.sp, 1)
-    v.wait_ge(T.sem.sp, len(done) + 16)
+        g.tensor.matmul(T.psb[:, u:256:8], s, T.inv[:, 0:DW:2], True, False).then_inc(T.sem.sp, 1)
+        g.tensor.matmul(T.psb[:, u:256:8], s, T.inv[:, 1:DW:2], False, True).then_inc(T.sem.sp, 1)
+    v.wait_ge(T.sem.sp, 8 + 16)
     noff = vi(v.tensor_copy(T.off[:], T.psb[:, 0:256]))
 
-    data = ["ld%d" % i for i in range(PIECES)] + ["%s%d" % (k, i) for k in ("x", "y") for i in range(PIECES)] + ["fin"]
+    data = ["ld%d" % i for i in range(NP)] + ["fw%d" % k for k in range(len(JOIN) - 1)] + ["fin"]
     for queue in (v, g.scalar):
         queue.wait_ge(T.sem.sv, noff)
         for s in data:
             queue.wait_ge(T.sem[s], total[core, s])
-    stores = 0
-    for i in range(H // GCH):
-        a = GCH * i
-        n = vi(v.tensor_copy(T.yb[:, a:a + GCH], T.win[:, 0:NR * R].indirect(T.off[:, a // 16:(a + GCH) // 16])))
+    stores, a = 0, 0
+    for i, w in enumerate(CHUNKS):
+        n = vi(v.tensor_copy(T.yb[:, a:a + w], T.win[:, 0:NR * R].indirect(T.off[:, a // 16:(a + w) // 16])))
         b = H + a
-        g.scalar.activation(T.yb[:, b:b + GCH], T.win[:, 0:NR * R].indirect(T.off[:, b // 16:(b + GCH) // 16]),
+        g.scalar.activation(T.yb[:, b:b + w], T.win[:, 0:NR * R].indirect(T.off[:, b // 16:(b + w) // 16]),
                             ActivationFunctionType.Identity, bias=T.nz[:, 0:1], scale=1.0).then_inc(T.sem.ss, 1)
         for sem, k, c in ((T.sem.sv, n, a), (T.sem.ss, i + 1, b)):
             g.sync.wait_ge(sem, k)
-            g.sync.dma_start(T.y[:, c:c + GCH], T.yb[:, c:c + GCH]).then_inc(T.sem.st, 16)
+            g.sync.dma_start(T.y[:, c:c + w], T.yb[:, c:c + w]).then_inc(T.sem.st, 16)
             stores += 16
+        a += w
     g.sync.wait_ge(T.sem.st, stores)
+    return made

from concourse.bass import DstId, RemoteDMATransfer
from concourse.mybir import dt, AluOpType, ActivationFunctionType

R = 4096
NR = 4
H = R // 2
SIZES = (256, 704, 640, 448)
NP = len(SIZES)
AT = [sum(SIZES[:i]) for i in range(NP + 1)]
JOIN = (0, 2, NP - 1)
CHUNKS = (832, 704, 512)
DW = 64

SCRATCH = {
    "win": ("sbuf", [128, NR * R], "bfloat16"),
    "yb": ("sbuf", [128, R], "bfloat16"),
    "lt": ("sbuf", [128, 16], "int32"),
    "ei": ("sbuf", [128, 32], "int32"),
    "eb": ("sbuf", [128, 16], "bfloat16"),
    "ab": ("sbuf", [128, 16], "bfloat16"),
    "oh": ("sbuf", [128, 8 * 128], "bfloat16"),
    "rh": ("sbuf", [128, 8 * 256], "bfloat16"),
    "i128": ("sbuf", [128, 128], "bfloat16"),
    "h128": ("sbuf", [128, 128], "bfloat16"),
    "iq": ("sbuf", [128, 128], "bfloat16"),
    "kc": ("sbuf", [128, 8], "bfloat16"),
    "own": ("sbuf", [128, DW], "bfloat16"),
    "sel": ("sbuf", [128, 8 * 128], "bfloat16"),
    "dd": ("sbuf", [128, NR * DW], "bfloat16"),
    "dr": ("sbuf", [128, NR * DW], "bfloat16"),
    "inv0": ("sbuf", [128, DW], "bfloat16"),
    "inv1": ("sbuf", [128, DW], "bfloat16"),
    "dfar": ("sbuf", [128, DW], "bfloat16"),
    "inv": ("sbuf", [128, DW], "bfloat16"),
    "off": ("sbuf", [128, 256], "uint16"),
    "nz": ("sbuf", [128, 1], "float32"),
    "psa": ("psum", [128, 512], "float32"),
    "psb": ("psum", [128, 512], "float32"),
}
SEMAPHORES = (["lst", "dd", "dn", "df", "fin", "sent", "sg", "sv", "ss", "sp", "st"]
              + ["%s%d" % (k, i) for k in ("ld", "x", "y", "fw") for i in range(NP)])


def bits(mask):
    return [1 << b for b in range(mask.bit_length()) if mask >> b & 1]


def part(mask, i, n):
    b = bits(mask)
    k = len(b) // n
    return sum(b[i * k:(i + 1) * k])


def roles(cores, topo):
    allc = range(topo.CHIPS * topo.CORES_PER_CHIP)
    out = {}
    for s in cores:
        mate = [c for c in cores if c != s and topo.chip(c) == topo.chip(s)][0]
        far = [c for c in cores if topo.chip(c) != topo.chip(s)]
        p = [c for c in far if topo.die(c) == topo.die(s)][0]
        q = [c for c in far if c != p][0]
        relay = [c for c in allc if topo.mates(topo.chip(c), topo.chip(p)) and topo.same_plane(topo.chip(c), topo.chip(s))
                 and topo.die(c) == topo.die(s) and topo.may_write(c, p) and topo.may_write(s, c)][0]
        port = [c for c in allc if topo.chip(c) == topo.chip(s) and topo.die(c) == topo.die(s)
                and c not in cores and topo.may_write(c, p)][0]
        out[s] = {"mate": mate, "p": p, "q": q, "relay": relay, "port": port}
    return out


def plan(cores, topo):
    ro = roles(cores, topo)
    calls, total = {}, {}

    def call(core, after, transfers):
        calls.setdefault(core, []).append((after, transfers))
        for t in transfers:
            total[t[0], t[2]] = total.get((t[0], t[2]), 0) + len(bits(t[1]))

    def win(dst, mask, sem, a, b):
        return (dst, mask, sem, "win", a, b, "win", a)

    for r, s in enumerate(cores):
        o = ro[s]
        mate, p, q, relay, port = o["mate"], o["p"], o["q"], o["relay"], o["port"]
        offm = topo.mask(s, relay)
        allm = topo.mask(s, mate)
        onm = allm & ~offm
        total[s, "lst"] = 32
        for i in range(NP):
            total[s, "ld%d" % i] = 32
        X = [(R * r + AT[i], R * r + AT[i + 1]) for i in range(NP)]
        Y = [(H + a, H + b) for a, b in X]

        def D(dst, mask, sem, d, buf, c):
            return (dst, mask, sem, "dd", DW * d, DW * d + DW, buf, c)

        rp, rq, rm = cores.index(p), cores.index(q), cores.index(mate)
        last = NP - 1
        for i in range(NP):
            if i == last:
                call(s, ["D"], [D(relay, part(offm, 0, 2), "dd", rp, "dd", DW * rp),
                                D(relay, part(offm, 1, 2), "dd", rq, "dd", DW * rq),
                                D(mate, onm, "dn", rm, "dr", DW * r)])
            call(s, ["ld%d" % i], [win(relay, offm, "y%d" % i, *Y[i]), win(port, onm, "x%d" % i, *X[i])])
        call(s, [], [win(mate, allm, "fin", Y[0][0], Y[-1][1])])
        pm, rm = topo.mask(port, p), topo.mask(relay, p)
        po = topo.mask(port, mate) & ~pm
        for k in range(len(JOIN) - 1):
            for i in range(JOIN[k], JOIN[k + 1]):
                if i == 0:
                    call(port, ["x0"], [win(p, pm, "fw0", *X[0])])
                    call(port, [], [win(mate, po, "fin", *X[0])])
                else:
                    call(port, ["x%d" % i], [win(p, pm, "fw%d" % k, *X[i]), win(mate, po, "fin", *X[i])])
                call(relay, ["y%d" % i], [win(p, rm, "fw%d" % k, *Y[i])])
        call(port, ["x%d" % last], [win(p, part(pm, 0, 2), "fin", *X[last]), win(q, part(pm, 1, 2), "fin", *X[last]),
                                    win(mate, po, "fin", *X[last])])
        call(relay, ["dd"], [D(p, part(rm, 0, 2), "df", rp, "dr", DW * r), D(q, part(rm, 1, 2), "df", rq, "dr", DW * r)])
        call(relay, ["y%d" % last], [win(p, part(rm, 0, 2), "fin", *Y[last]), win(q, part(rm, 1, 2), "fin", *Y[last])])
    for r, s in enumerate(cores):
        p, q = ro[s]["p"], ro[s]["q"]
        m = topo.mask(p, q)
        for k in range(len(JOIN) - 1):
            a, b = R * r + AT[JOIN[k]], R * r + AT[JOIN[k + 1]]
            call(p, ["fw%d" % k], [win(q, part(m, 0, 2), "fin", a, b), win(q, part(m, 1, 2), "fin", H + a, H + b)])
    return calls, total


def rank_program(g, core, T, topo):
    cores = list(T.cores)
    calls, total = plan(cores, topo)
    rank = T.rank_of(core)
    if rank is None and core not in calls:
        return
    made = 0
    if rank is not None:
        near = [r for r in range(NR) if topo.chip(cores[r]) == topo.chip(core) and r != rank]
        far = [r for r in range(NR) if topo.chip(cores[r]) != topo.chip(core)]
        made = compute(g, core, rank, near[0], far, T, total)
    sent = 0
    for after, transfers in calls[core]:
        for sem in after:
            if sem == "D":
                g.wait_ge(T.sem.sv, made)
            else:
                g.wait_ge(T.sem[sem], total[core, sem])
        ts = []
        for d, m, sem, buf, a, b, dbuf, da in transfers:
            rid, pid, _ = topo.addr(d)
            ts.append(RemoteDMATransfer(dst_ids=[DstId(rid=rid, pnc=pid)], dma_engine_mask=m, remote_sem=T.sem[sem],
                                        src=T[buf][:, a:b], dst=T[dbuf][:, da:da + b - a]))
            sent += len(bits(m))
        g.remote_dma_fused(ts, local_sem=T.sem.sent)
    g.wait_ge(T.sem.sent, sent)


def compute(g, core, rank, near, far, T, total):
    A = AluOpType
    v, base = g.vector, R * rank
    g.sync.dma_start(T.lt[:, 0:8], T.src[:]).then_inc(T.sem.lst, 16)
    g.scalar.dma_start(T.lt[:, 8:16], T.dst[:]).then_inc(T.sem.lst, 16)
    for i in range(NP):
        for queue, o in ((g.sync, 0), (g.scalar, H)):
            a, b = o + AT[i], o + AT[i + 1]
            queue.dma_start(T.win[:, base + a:base + b], T.tab[:, a:b]).then_inc(T.sem["ld%d" % i], 16)
    g.iota(T.i128[:], [[1, 128]], 0, 0, allow_small_or_imprecise_dtypes=True).then_inc(T.sem.sg, 1)
    g.iota(T.kc[:], [[-16, 8]], 0, 1, allow_small_or_imprecise_dtypes=True).then_inc(T.sem.sg, 1)
    g.iota(T.iq[:], [[0, 8], [1, 16]], 0, 0, allow_small_or_imprecise_dtypes=True).then_inc(T.sem.sg, 1)

    vn = [0]

    def vi(ins):
        vn[0] += 1
        ins.then_inc(T.sem.sv, 1)
        return vn[0]

    def vwait():
        v.wait_ge(T.sem.sv, vn[0])

    vi(v.memset(T.nz[:], -0.0))
    v.wait_ge(T.sem.sg, 3)
    vi(v.tensor_scalar(T.h128[:], T.i128[:], 128.0, None, A.mult))
    for u in range(8):
        vi(v.tensor_scalar(T.sel[:, 128 * u:128 * u + 128], T.iq[:], T.kc[:, u:u + 1], None, A.is_equal))
    vwait()
    vi(v.tensor_copy(T.own[:, 0:DW:2], T.h128[:, 32 * rank:32 * rank + 32]))
    vi(v.tensor_scalar(T.own[:, 1:DW:2], T.h128[:, 0:32], 0.0, T.kc[:, 0:1], A.mult, A.add))
    v.wait_ge(T.sem.lst, total[core, "lst"])
    vi(v.tensor_scalar(T.ei[:, 0:32:2], T.lt[:], 127, None, A.bitwise_and))
    vi(v.tensor_scalar(T.ei[:, 1:32:2], T.lt[:], (NR * R - 1) & ~127, None, A.bitwise_and))
    vwait()
    vi(v.tensor_copy(T.eb[:], T.ei[:, 16:32]))
    vi(v.tensor_tensor(T.ab[:], T.ei[:, 0:16], T.ei[:, 16:32], A.subtract))
    vwait()
    for t in range(8):
        lo, hi, c = 2 * t, 2 * t + 1, 256 * t
        vi(v.tensor_scalar(T.oh[:, 128 * t:128 * t + 128], T.i128[:], T.eb[:, lo:lo + 1], None, A.is_equal))
        vi(v.tensor_scalar(T.rh[:, c:c + 256:2], T.h128[:], T.eb[:, hi:hi + 1], T.ab[:, hi:hi + 1], A.is_equal, A.mult))
        n = vi(v.tensor_scalar(T.rh[:, c + 1:c + 256:2], T.h128[:], T.eb[:, hi:hi + 1], T.ab[:, lo:lo + 1],
                               A.is_equal, A.mult))
        g.tensor.wait_ge(T.sem.sv, n)
        g.tensor.matmul(T.psa[:, 0:256], T.oh[:, 128 * t:128 * t + 128], T.rh[:, c:c + 256],
                        t == 0, t == 7).then_inc(T.sem.sp, 1)
    v.wait_ge(T.sem.sp, 8)
    made = vi(v.tensor_copy(T.dd[:], T.psa[:, 0:256]))
    vwait()

    def mine(r):
        return T.dr[:, DW * r:DW * r + DW]

    vi(v.tensor_tensor(T.inv0[:], T.dd[:, DW * rank:DW * rank + DW], T.own[:], A.add))
    vwait()
    v.wait_ge(T.sem.dn, total[core, "dn"])
    vi(v.tensor_tensor(T.inv1[:], T.inv0[:], mine(near), A.add))
    v.wait_ge(T.sem.df, total[core, "df"])
    vi(v.tensor_tensor(T.dfar[:], mine(far[0]), mine(far[1]), A.add))
    vwait()
    n = vi(v.tensor_tensor(T.inv[:], T.inv1[:], T.dfar[:], A.add))
    g.tensor.wait_ge(T.sem.sv, n)
    for u in range(8):
        s = T.sel[:, 128 * u:128 * u + 128]
        g.tensor.matmul(T.psb[:, u:256:8], s, T.inv[:, 0:DW:2], True, False).then_inc(T.sem.sp, 1)
        g.tensor.matmul(T.psb[:, u:256:8], s, T.inv[:, 1:DW:2], False, True).then_inc(T.sem.sp, 1)
    v.wait_ge(T.sem.sp, 8 + 16)
    noff = vi(v.tensor_copy(T.off[:], T.psb[:, 0:256]))

    data = ["ld%d" % i for i in range(NP)] + ["fw%d" % k for k in range(len(JOIN) - 1)] + ["fin"]
    for queue in (v, g.scalar):
        queue.wait_ge(T.sem.sv, noff)
        for s in data:
            queue.wait_ge(T.sem[s], total[core, s])
    stores, a = 0, 0
    for i, w in enumerate(CHUNKS):
        n = vi(v.tensor_copy(T.yb[:, a:a + w], T.win[:, 0:NR * R].indirect(T.off[:, a // 16:(a + w) // 16])))
        b = H + a
        g.scalar.activation(T.yb[:, b:b + w], T.win[:, 0:NR * R].indirect(T.off[:, b // 16:(b + w) // 16]),
                            ActivationFunctionType.Identity, bias=T.nz[:, 0:1], scale=1.0).then_inc(T.sem.ss, 1)
        for sem, k, c in ((T.sem.sv, n, a), (T.sem.ss, i + 1, b)):
            g.sync.wait_ge(sem, k)
            g.sync.dma_start(T.y[:, c:c + w], T.yb[:, c:c + w]).then_inc(T.sem.st, 16)
            stores += 16
        a += w
    g.sync.wait_ge(T.sem.st, stores)
    return made
